import numpy as np
import ml_dtypes


def mxq(x, axis, fmt="e4m3"):
    dtype, down = {"e4m3": (ml_dtypes.float8_e4m3fn, 7), "e5m2": (ml_dtypes.float8_e5m2, 14)}[fmt]
    v = np.moveaxis(np.asarray(x, np.float32).astype(ml_dtypes.bfloat16).astype(np.float64), axis, -1)
    blocks = v.reshape(v.shape[:-1] + (-1, 32))
    amax = np.abs(blocks).max(-1, keepdims=True)
    byte = np.maximum(np.where(amax > 0, np.frexp(amax)[1] - 1 + 127, 0) - down, 1)
    scale = np.exp2(byte - 127.0)
    codes = (blocks / scale).astype(np.float32).astype(dtype).astype(np.float64)
    return np.moveaxis((codes * scale).reshape(v.shape), -1, axis)


WIDE = False


def mx_kscale(k):
    if not WIDE:
        return np.ones(k)
    levels = np.array([10, -10, 5, -5, 0])
    if k % 512:
        return np.exp2(np.random.permutation(np.resize(levels, k // 32))).repeat(32)
    a = np.empty((k // 512, 16))
    for p in range(k // 512):
        a[p, :8] = np.random.permutation(np.resize(levels, 8))
        for g in range(8):
            far = levels[np.abs(levels - a[p, g]) >= 10]
            a[p, g + 8] = far[np.random.randint(len(far))]
    return np.exp2(a.ravel()).repeat(32)


def f64(x):
    return np.asarray(x).astype(np.float64)


def striped(idx):
    return np.tile(np.asarray(idx).reshape(-1, 16).T, (8, 1)).astype(np.uint16)


def unstriped(offs):
    return offs[:16].T.reshape(-1).astype(np.int64)


def striped8(idx):
    return np.asarray(idx).reshape(8, -1, 16).transpose(0, 2, 1).reshape(128, -1).astype(np.uint16)


def unstriped8(offs):
    return offs.reshape(8, 16, -1).transpose(0, 2, 1).reshape(8, -1).astype(np.int64)


def pick8(x, idx, run):
    r = np.arange(len(x))
    return x[r[:, None], idx[r % (8 * run) // run]]


E2M1 = np.array([0.0, 0.5, 1.0, 1.5, 2.0, 3.0, 4.0, 6.0, -0.0, -0.5, -1.0, -1.5, -2.0, -3.0, -4.0, -6.0])


def pack_weight(w, fmt):
    k, n = w.shape
    w = f64(np.asarray(w, np.float32).astype(ml_dtypes.bfloat16)).reshape(k // 32, 32, n)
    amax = np.abs(w).max(1)
    if fmt == "e4m3":
        byte = np.frexp(amax)[1] - 1 + 127 - 7
    else:
        mant, ex = np.frexp(amax / 6.0)
        byte = np.where(mant > 0.5, ex, ex - 1) + 127
    byte = np.clip(np.where(amax > 0, byte, 1), 1, 254)
    scaled = (w * np.exp2(127.0 - byte)[:, None, :]).reshape(k, n).astype(np.float32)
    by_word = np.ascontiguousarray(scaled.reshape(k // 512, 128, 4, n).transpose(0, 1, 3, 2))
    if fmt == "e4m3":
        words = by_word.astype(ml_dtypes.float8_e4m3fn).view(np.uint8)
    else:
        c = by_word.astype(ml_dtypes.float4_e2m1fn).view(np.uint8) & 0xF
        words = (c[..., 0::2] | (c[..., 1::2] << 4)).reshape(k // 512, 128, 2 * n)
    return np.ascontiguousarray(words), np.ascontiguousarray(byte.astype(np.uint8).reshape(k // 512, 16, n))


def unpack_weight(words, scales, fmt):
    g, _, n = scales.shape
    words = np.ascontiguousarray(words).reshape(g, 128, n, -1)
    if fmt == "e4m3":
        vals = words.view(ml_dtypes.float8_e4m3fn).astype(np.float64)
    else:
        nib = np.empty((g, 128, n, 4), np.uint8)
        nib[..., 0::2] = words & 0xF
        nib[..., 1::2] = words >> 4
        vals = E2M1[nib]
    vals = vals * np.repeat(np.exp2(scales.astype(np.float64) - 127.0), 8, axis=1)[..., None]
    return vals.transpose(0, 1, 3, 2).reshape(g * 512, n)


K, J, R, T, F, C, S, N = 512, 256, 512, 1024, 1024, 512, 128, 256


def setup_inputs():
    n = np.random.standard_normal
    idx = np.random.permutation(T)[:J]
    idx2 = np.random.permutation(F)[:R]
    idx3 = np.stack([np.random.permutation(C)[:J] for _ in range(8)])
    idx4 = np.stack([np.random.permutation(J)[:S] for _ in range(8)])
    idx5 = np.stack([np.random.permutation(C)[:S] for _ in range(8)])
    idx6 = np.random.permutation(T)[:C]
    fk = mx_kscale(K)
    fr = mx_kscale(R)
    tr = np.ones(F)
    tr[idx2] = fr
    xtp = pack_weight(n((K, T)) * fk[:, None], "e2m1")
    wtp = pack_weight(n((K, F)) * 1 / np.sqrt(K) / fk[:, None] * tr, "e4m3")
    wbp = pack_weight(n((R, N)) * 1 / np.sqrt(R) / fr[:, None], "e2m1")
    wsp = pack_weight(n((K, N)) * 1 / np.sqrt(K) / fk[:, None], "e4m3")
    return {
        "xt_words": xtp[0],
        "xt_scales": xtp[1],
        "wt_words": wtp[0],
        "wt_scales": wtp[1],
        "sa": (np.random.uniform(0.5, 1.6, (R, 1))).astype(np.float32),
        "wb_words": wbp[0],
        "wb_scales": wbp[1],
        "ws_words": wsp[0],
        "ws_scales": wsp[1],
        "offs": striped(idx),
        "offs2": striped(idx2),
        "offs3": striped8(idx3),
        "offs4": striped8(idx4),
        "offs5": striped8(idx5),
        "offs6": striped(idx6),
    }


def reference(xt_words, xt_scales, wt_words, wt_scales, sa, wb_words, wb_scales, ws_words, ws_scales, offs, offs2, offs3, offs4, offs5, offs6):
    idx = unstriped(offs)
    idx2 = unstriped(offs2)
    idx3 = unstriped8(offs3)
    idx4 = unstriped8(offs4)
    idx5 = unstriped8(offs5)
    idx6 = unstriped(offs6)
    xtu = unpack_weight(xt_words, xt_scales, "e2m1")
    wtu = unpack_weight(wt_words, wt_scales, "e4m3")
    wbu = unpack_weight(wb_words, wb_scales, "e2m1")
    wsu = unpack_weight(ws_words, ws_scales, "e4m3")
    wtidx2g = wtu[:, idx2]
    xtidxg = xtu[:, idx]
    a = wtidx2g.T @ xtidxg
    pw = np.zeros((R, C))
    pw[np.arange(R)[:, None], idx3[np.arange(R) % 512 // 64]] = a
    h1 = pick8(a, idx4, 64) * f64(sa)
    pv = np.zeros((R, C))
    pv[np.arange(R)[:, None], idx5[np.arange(R) % 512 // 64]] = h1
    hid = np.abs(pw - pv)
    hidq = mxq(hid, 0, "e4m3")
    xtidx6g = xtu[:, idx6]
    y = wbu.T @ hidq + wsu.T @ xtidx6g
    return y

@@ -1,0 +1,204 @@
+from contextlib import ExitStack
+
+import concourse.mybir as mybir
+
+K, J, R, T, F, C, S, N = 512, 256, 512, 1024, 1024, 512, 128, 256
+FLOPS = 2 * K * R * J + 2 * R * N * C + 2 * K * N * C
+
+F32 = mybir.dt.float32
+BF16 = mybir.dt.bfloat16
+I32 = mybir.dt.int32
+U32 = mybir.dt.uint32
+U16 = mybir.dt.uint16
+U8 = mybir.dt.uint8
+FP8X4 = mybir.dt.float8_e4m3fn_x4
+FP4X4 = mybir.dt.float4_e2m1fn_x4
+ACT = mybir.ActivationFunctionType
+ALU = mybir.AluOpType
+
+P = 128
+PACK = 4
+QUADS = 4
+GROUP = 16
+HALF = J // 2
+CHUNK = 128
+CHUNKS = C // CHUNK
+
+
+def tile_picked_tokens_store_one_overlay_further_plain_kernel(
+    tc, xt_words, xt_scales, wt_words, wt_scales, sa, wb_words, wb_scales, ws_words, ws_scales,
+    offs, offs2, offs3, offs4, offs5, offs6, out,
+):
+    nc = tc.nc
+    with ExitStack() as ctx:
+        lists = ctx.enter_context(tc.tile_pool(name="lists", bufs=1))
+        keep = ctx.enter_context(tc.tile_pool(name="keep", bufs=1))
+        psum = ctx.enter_context(tc.psum_pool(name="psum", bufs=1))
+
+        def load_list(src, name):
+            tile = lists.tile(list(src.shape), U16, name=name)
+            nc.sync.dma_start(tile[:], src)
+            return tile
+
+        def cleared_plane(width, name):
+            plane = keep.tile([P, width], U8, name=name, align_bytes=64)
+            nc.vector.memset(plane[:].bitcast(I32), 0)
+            return plane
+
+        def load_scale_rows(plane, scales):
+            for q in range(QUADS):
+                nc.sync.dma_start(
+                    plane[32 * q : 32 * q + 4, :].bitcast(I32), scales[0, 4 * q : 4 * q + 4, :].bitcast(I32)
+                )
+
+        wt_s = cleared_plane(F, "wt_s")
+        xt_s = cleared_plane(T, "xt_s")
+        feat_list = load_list(offs2, "feat_list")
+        wt_w = keep.tile([P, F], U32, name="wt_w", align_bytes=64)
+        nc.sync.dma_start(wt_w[:].bitcast(I32), wt_words[0].rearrange("p n t -> p (n t)").bitcast(I32))
+        load_scale_rows(wt_s, wt_scales)
+        slot_list = load_list(offs, "slot_list")
+        xt_w = keep.tile([P, T], U16, name="xt_w", align_bytes=64)
+        nc.sync.dma_start(xt_w[:].bitcast(I32), xt_words[0].bitcast(I32))
+        load_scale_rows(xt_s, xt_scales)
+        board_list = load_list(offs3, "board_list")
+        pick_list = load_list(offs4, "pick_list")
+        weight = keep.tile([P, PACK], F32, name="weight")
+        nc.sync.dma_start(weight[:], sa.rearrange("(p t) o -> p (t o)", t=PACK))
+        overlay_list = load_list(offs5, "overlay_list")
+        column_list = load_list(offs6, "column_list")
+
+        boards = [keep.tile([P, C], F32, name=f"board{i}") for i in range(2)]
+        overlays = [keep.tile([P, C], F32, name=f"overlay{i}") for i in range(2)]
+        for tile in boards + overlays:
+            nc.vector.memset(tile[:], 0.0)
+
+        ws_s = cleared_plane(N, "ws_s")
+        wb_s = cleared_plane(N, "wb_s")
+        ws_w = keep.tile([P, N], U32, name="ws_w", align_bytes=64)
+        nc.sync.dma_start(ws_w[:].bitcast(I32), ws_words[0].rearrange("p n t -> p (n t)").bitcast(I32))
+        load_scale_rows(ws_s, ws_scales)
+        wb_w = keep.tile([P, N], U16, name="wb_w", align_bytes=64)
+        nc.sync.dma_start(wb_w[:].bitcast(I32), wb_words[0].bitcast(I32))
+        load_scale_rows(wb_s, wb_scales)
+
+        feat_s = keep.tile([P, PACK, P], U8, name="feat_s", align_bytes=64)
+        feat_w = keep.tile([P, PACK, P], U32, name="feat_w", align_bytes=64)
+        nc.vector.tensor_copy(feat_s[:].rearrange("p t m -> p m t"), wt_s[:].indirect(feat_list[:]))
+        nc.vector.tensor_copy(feat_w[:].rearrange("p t m -> p m t"), wt_w[:].indirect(feat_list[:]))
+
+        hidden = [keep.tile([P, J], F32, name=f"hidden{t}") for t in range(PACK)]
+        slot_w = keep.tile([P, J], U16, name="slot_w", align_bytes=64)
+        slot_s = keep.tile([P, J], U8, name="slot_s", align_bytes=64)
+
+        def hidden_product(t, cols, bank):
+            acc = psum.tile([P, cols.stop - cols.start], F32, name=f"acc_{t}_{cols.start}", tag=f"first{bank}")
+            nc.tensor.matmul_mx(
+                out=acc[:], lhsT=feat_w[:, t, :].bitcast(FP8X4), lhsT_scale=feat_s[:, t, :],
+                rhs=slot_w[:, cols].bitcast(FP4X4), rhs_scale=slot_s[:, cols], start=True, stop=True,
+            )
+            return acc
+
+        halves = [slice(h * HALF, (h + 1) * HALF) for h in range(2)]
+        for h, cols in enumerate(halves):
+            entries = slot_list[:, cols.start // GROUP : cols.stop // GROUP]
+            nc.vector.tensor_copy(slot_w[:, cols], xt_w[:].indirect(entries))
+            nc.vector.tensor_copy(slot_s[:, cols], xt_s[:].indirect(entries))
+            for t in range(2):
+                acc = hidden_product(t, cols, 2 * h + t)
+                if h == 0 and t == 0:
+                    nc.scalar.copy(hidden[t][:, cols], acc[:])
+                else:
+                    nc.vector.tensor_copy(hidden[t][:, cols], acc[:])
+        for t in range(2, PACK):
+            acc = hidden_product(t, slice(0, J), t - 2)
+            nc.vector.tensor_copy(hidden[t][:], acc[:])
+
+        col_w = keep.tile([P, C], U16, name="col_w", align_bytes=64)
+        col_s = keep.tile([P, C], U8, name="col_s", align_bytes=64)
+        nc.vector.tensor_copy(col_w[:], xt_w[:].indirect(column_list[:]))
+        nc.vector.tensor_copy(col_s[:], xt_s[:].indirect(column_list[:]))
+        chunks = [slice(i * CHUNK, (i + 1) * CHUNK) for i in range(CHUNKS)]
+        sums = [psum.tile([P, N // P, CHUNK], F32, name=f"sum{i}") for i in range(CHUNKS)]
+        for i, cols in enumerate(chunks):
+            for u in range(N // P):
+                rows = slice(u * P, (u + 1) * P)
+                nc.tensor.matmul_mx(
+                    out=sums[i][:, u, :], lhsT=ws_w[:, rows].bitcast(FP8X4), lhsT_scale=ws_s[:, rows],
+                    rhs=col_w[:, cols].bitcast(FP4X4), rhs_scale=col_s[:, cols], start=(u == 0), stop=False,
+                )
+
+        picked = [keep.tile([P, S], F32, name=f"picked{t}") for t in range(PACK)]
+
+        def put_board(t, cols):
+            entries = board_list[:, cols.start // GROUP : cols.stop // GROUP]
+            nc.scalar.activation(boards[t % 2][:].indirect(entries), hidden[t][:, cols], ACT.Copy)
+
+        def pick(t):
+            nc.scalar.activation(
+                picked[t][:], hidden[t][:].indirect(pick_list[:]), ACT.Copy, scale=weight[:, t : t + 1]
+            )
+
+        def put_overlay(t):
+            nc.scalar.activation(overlays[t % 2][:].indirect(overlay_list[:]), picked[t][:], ACT.Copy)
+
+        diffs = [keep.tile([P, 2, C], F32, name=f"diff{u}") for u in range(2)]
+        hid = keep.tile([P, C, PACK], BF16, name="hid", align_bytes=64)
+
+        def subtract(t, cols):
+            nc.vector.tensor_tensor(
+                diffs[t // 2][:, t % 2, cols], boards[t % 2][:, cols], overlays[t % 2][:, cols], ALU.subtract
+            )
+
+        def magnitude_on_vector(u, cols):
+            pair = diffs[u][:, :, cols].rearrange("p e c -> p c e")
+            nc.vector.scalar_tensor_tensor(hid[:, cols, 2 * u : 2 * u + 2], pair, -1.0, pair, ALU.mult, ALU.max)
+
+        def magnitude_on_scalar(u, cols):
+            pair = diffs[u][:, :, cols].rearrange("p e c -> p c e")
+            nc.scalar.activation(hid[:, cols, 2 * u : 2 * u + 2], pair, ACT.Abs)
+
+        whole = slice(0, C)
+        for cols in halves:
+            put_board(0, cols)
+            put_board(1, cols)
+        pick(0)
+        pick(1)
+        for t in range(2):
+            put_overlay(t)
+            subtract(t, whole)
+        magnitude_on_vector(0, whole)
+        pick(2)
+        put_board(2, slice(0, J))
+        put_overlay(2)
+        subtract(2, whole)
+        pick(3)
+        put_board(3, slice(0, J))
+        put_overlay(3)
+        for cols in chunks:
+            subtract(3, cols)
+        for i, cols in enumerate(chunks):
+            if i < CHUNKS - 1:
+                magnitude_on_scalar(1, cols)
+            else:
+                magnitude_on_vector(1, cols)
+
+        out_view = out.rearrange("(u p) c -> p u c", p=P)
+        for i, cols in enumerate(chunks):
+            hid_w = keep.tile([P, CHUNK], U32, name=f"hid_w{i}", align_bytes=64)
+            hid_s = keep.tile([P, CHUNK], U8, name=f"hid_s{i}", align_bytes=64)
+            nc.vector.quantize_mx(
+                out=hid_w[:].bitcast(FP8X4), scales=hid_s[:], in_=hid[:, cols, :].rearrange("p c t -> p (c t)")
+            )
+            for u in range(N // P):
+                rows = slice(u * P, (u + 1) * P)
+                nc.tensor.matmul_mx(
+                    out=sums[i][:, u, :], lhsT=wb_w[:, rows].bitcast(FP4X4), lhsT_scale=wb_s[:, rows],
+                    rhs=hid_w[:].bitcast(FP8X4), rhs_scale=hid_s[:], start=False, stop=(u == N // P - 1),
+                )
+            result = keep.tile([P, N // P, CHUNK], F32, name=f"result{i}")
+            if i % 2 == 0:
+                nc.scalar.copy(result[:], sums[i][:])
+            else:
+                nc.vector.tensor_copy(result[:], sums[i][:])
+            nc.sync.dma_start(out_view[:, :, cols], result[:])

@@ -22,6 +22,7 @@ QUADS = 4
 GROUP = 16
 HALF = J // 2
 CHUNK = 128
+RING = 3
 CHUNKS = C // CHUNK
 
 
@@ -42,7 +43,7 @@ def tile_picked_tokens_store_one_overlay_further_plain_kernel(
 
         def cleared_plane(width, name):
             plane = keep.tile([P, width], U8, name=name, align_bytes=64)
-            nc.vector.memset(plane[:].bitcast(I32), 0)
+            nc.gpsimd.memset(plane[:].bitcast(I32), 0)
             return plane
 
         def load_scale_rows(plane, scales):
@@ -51,16 +52,24 @@ def tile_picked_tokens_store_one_overlay_further_plain_kernel(
                     plane[32 * q : 32 * q + 4, :].bitcast(I32), scales[0, 4 * q : 4 * q + 4, :].bitcast(I32)
                 )
 
-        wt_s = cleared_plane(F, "wt_s")
-        xt_s = cleared_plane(T, "xt_s")
-        feat_list = load_list(offs2, "feat_list")
+        def load_scale_window(plane, scales, queues):
+            for q, queue in enumerate(queues):
+                rows = scales[0, 4 * q : 4 * q + 4, :].bitcast(I32)
+                queue.dma_start(
+                    plane[32 * q : 32 * q + 32, :].bitcast(I32),
+                    rows.unsqueeze(0).broadcast_to([8, 4, scales.shape[2] // 4]),
+                )
+
+        wt_s = keep.tile([P, F], U8, name="wt_s", align_bytes=64)
         wt_w = keep.tile([P, F], U32, name="wt_w", align_bytes=64)
-        nc.sync.dma_start(wt_w[:].bitcast(I32), wt_words[0].rearrange("p n t -> p (n t)").bitcast(I32))
-        load_scale_rows(wt_s, wt_scales)
-        slot_list = load_list(offs, "slot_list")
+        xt_s = keep.tile([P, T], U8, name="xt_s", align_bytes=64)
         xt_w = keep.tile([P, T], U16, name="xt_w", align_bytes=64)
+        feat_list = load_list(offs2, "feat_list")
+        load_scale_window(wt_s, wt_scales, [nc.scalar, nc.sync, nc.scalar, nc.sync])
+        nc.sync.dma_start(wt_w[:].bitcast(I32), wt_words[0].rearrange("p n t -> p (n t)").bitcast(I32))
         nc.sync.dma_start(xt_w[:].bitcast(I32), xt_words[0].bitcast(I32))
-        load_scale_rows(xt_s, xt_scales)
+        load_scale_window(xt_s, xt_scales, [nc.sync] * QUADS)
+        slot_list = load_list(offs, "slot_list")
         board_list = load_list(offs3, "board_list")
         pick_list = load_list(offs4, "pick_list")
         weight = keep.tile([P, PACK], F32, name="weight")
@@ -68,10 +77,12 @@ def tile_picked_tokens_store_one_overlay_further_plain_kernel(
         overlay_list = load_list(offs5, "overlay_list")
         column_list = load_list(offs6, "column_list")
 
-        boards = [keep.tile([P, C], F32, name=f"board{i}") for i in range(2)]
-        overlays = [keep.tile([P, C], F32, name=f"overlay{i}") for i in range(2)]
-        for tile in boards + overlays:
-            nc.vector.memset(tile[:], 0.0)
+        boards = [keep.tile([P, C], F32, name=f"board{i}") for i in range(RING)]
+        overlays = [keep.tile([P, C], F32, name=f"overlay{i}") for i in range(RING)]
+        for i in range(RING):
+            engine = nc.gpsimd if i == RING - 1 else nc.vector
+            engine.memset(boards[i][:], 0.0)
+            engine.memset(overlays[i][:], 0.0)
 
         ws_s = cleared_plane(N, "ws_s")
         wb_s = cleared_plane(N, "wb_s")
@@ -119,20 +130,28 @@ def tile_picked_tokens_store_one_overlay_further_plain_kernel(
         nc.vector.tensor_copy(col_w[:], xt_w[:].indirect(column_list[:]))
         nc.vector.tensor_copy(col_s[:], xt_s[:].indirect(column_list[:]))
         chunks = [slice(i * CHUNK, (i + 1) * CHUNK) for i in range(CHUNKS)]
-        sums = [psum.tile([P, N // P, CHUNK], F32, name=f"sum{i}") for i in range(CHUNKS)]
+        shared = [psum.tile([P, N // P, CHUNK], F32, name=f"sum{i}") for i in range(CHUNKS - 1)]
+        last = [
+            psum.tile([P, CHUNK], F32, name="last0", tag="last0"),
+            psum.tile([P, CHUNK], F32, name="last1", tag="first2"),
+        ]
+
+        def sum_of(i, u):
+            return shared[i][:, u, :] if i < CHUNKS - 1 else last[u][:]
+
         for i, cols in enumerate(chunks):
             for u in range(N // P):
                 rows = slice(u * P, (u + 1) * P)
                 nc.tensor.matmul_mx(
-                    out=sums[i][:, u, :], lhsT=ws_w[:, rows].bitcast(FP8X4), lhsT_scale=ws_s[:, rows],
-                    rhs=col_w[:, cols].bitcast(FP4X4), rhs_scale=col_s[:, cols], start=(u == 0), stop=False,
+                    out=sum_of(i, u), lhsT=ws_w[:, rows].bitcast(FP8X4), lhsT_scale=ws_s[:, rows],
+                    rhs=col_w[:, cols].bitcast(FP4X4), rhs_scale=col_s[:, cols], start=(u == 0 or i == CHUNKS - 1), stop=False,
                 )
 
         picked = [keep.tile([P, S], F32, name=f"picked{t}") for t in range(PACK)]
 
         def put_board(t, cols):
             entries = board_list[:, cols.start // GROUP : cols.stop // GROUP]
-            nc.scalar.activation(boards[t % 2][:].indirect(entries), hidden[t][:, cols], ACT.Copy)
+            nc.scalar.activation(boards[t % RING][:].indirect(entries), hidden[t][:, cols], ACT.Copy)
 
         def pick(t):
             nc.scalar.activation(
@@ -140,25 +159,25 @@ def tile_picked_tokens_store_one_overlay_further_plain_kernel(
             )
 
         def put_overlay(t):
-            nc.scalar.activation(overlays[t % 2][:].indirect(overlay_list[:]), picked[t][:], ACT.Copy)
+            nc.scalar.activation(overlays[t % RING][:].indirect(overlay_list[:]), picked[t][:], ACT.Copy)
 
-        diffs = [keep.tile([P, 2, C], F32, name=f"diff{u}") for u in range(2)]
-        hid = keep.tile([P, C, PACK], BF16, name="hid", align_bytes=64)
+        diffs = [[keep.tile([P, 2, CHUNK], F32, name=f"diff{u}_{i}") for i in range(CHUNKS)] for u in range(2)]
+        hid = [keep.tile([P, CHUNK, PACK], BF16, name=f"hid{i}", align_bytes=64) for i in range(CHUNKS)]
 
-        def subtract(t, cols):
-            nc.vector.tensor_tensor(
-                diffs[t // 2][:, t % 2, cols], boards[t % 2][:, cols], overlays[t % 2][:, cols], ALU.subtract
-            )
+        def subtract(t):
+            for i, cols in enumerate(chunks):
+                nc.vector.tensor_tensor(
+                    diffs[t // 2][i][:, t % 2, :], boards[t % RING][:, cols], overlays[t % RING][:, cols], ALU.subtract
+                )
 
-        def magnitude_on_vector(u, cols):
-            pair = diffs[u][:, :, cols].rearrange("p e c -> p c e")
-            nc.vector.scalar_tensor_tensor(hid[:, cols, 2 * u : 2 * u + 2], pair, -1.0, pair, ALU.mult, ALU.max)
+        def magnitude_on_vector(u, i):
+            pair = diffs[u][i][:].rearrange("p e c -> p c e")
+            nc.vector.scalar_tensor_tensor(hid[i][:, :, 2 * u : 2 * u + 2], pair, -1.0, pair, ALU.mult, ALU.max)
 
-        def magnitude_on_scalar(u, cols):
-            pair = diffs[u][:, :, cols].rearrange("p e c -> p c e")
-            nc.scalar.activation(hid[:, cols, 2 * u : 2 * u + 2], pair, ACT.Abs)
+        def magnitude_on_scalar(u, i):
+            pair = diffs[u][i][:].rearrange("p e c -> p c e")
+            nc.scalar.activation(hid[i][:, :, 2 * u : 2 * u + 2], pair, ACT.Abs)
 
-        whole = slice(0, C)
         for cols in halves:
             put_board(0, cols)
             put_board(1, cols)
@@ -166,39 +185,48 @@ def tile_picked_tokens_store_one_overlay_further_plain_kernel(
         pick(1)
         for t in range(2):
             put_overlay(t)
-            subtract(t, whole)
-        magnitude_on_vector(0, whole)
-        pick(2)
-        put_board(2, slice(0, J))
-        put_overlay(2)
-        subtract(2, whole)
-        pick(3)
-        put_board(3, slice(0, J))
-        put_overlay(3)
-        for cols in chunks:
-            subtract(3, cols)
-        for i, cols in enumerate(chunks):
-            if i < CHUNKS - 1:
-                magnitude_on_scalar(1, cols)
-            else:
-                magnitude_on_vector(1, cols)
-
+            subtract(t)
+        for i in range(CHUNKS):
+            magnitude_on_vector(0, i)
+        for t in range(2, PACK):
+            pick(t)
+            put_board(t, slice(0, J))
+            put_overlay(t)
+            subtract(t)
         out_view = out.rearrange("(u p) c -> p u c", p=P)
-        for i, cols in enumerate(chunks):
+
+        def finish(i):
             hid_w = keep.tile([P, CHUNK], U32, name=f"hid_w{i}", align_bytes=64)
             hid_s = keep.tile([P, CHUNK], U8, name=f"hid_s{i}", align_bytes=64)
             nc.vector.quantize_mx(
-                out=hid_w[:].bitcast(FP8X4), scales=hid_s[:], in_=hid[:, cols, :].rearrange("p c t -> p (c t)")
+                out=hid_w[:].bitcast(FP8X4), scales=hid_s[:], in_=hid[i][:].rearrange("p c t -> p (c t)")
             )
             for u in range(N // P):
                 rows = slice(u * P, (u + 1) * P)
                 nc.tensor.matmul_mx(
-                    out=sums[i][:, u, :], lhsT=wb_w[:, rows].bitcast(FP4X4), lhsT_scale=wb_s[:, rows],
-                    rhs=hid_w[:].bitcast(FP8X4), rhs_scale=hid_s[:], start=False, stop=(u == N // P - 1),
+                    out=sum_of(i, u), lhsT=wb_w[:, rows].bitcast(FP4X4), lhsT_scale=wb_s[:, rows],
+                    rhs=hid_w[:].bitcast(FP8X4), rhs_scale=hid_s[:], start=False, stop=(u == N // P - 1 or i == CHUNKS - 1),
                 )
+
+        def store(i, copy):
             result = keep.tile([P, N // P, CHUNK], F32, name=f"result{i}")
-            if i % 2 == 0:
-                nc.scalar.copy(result[:], sums[i][:])
+            copy(result[:], shared[i][:])
+            nc.sync.dma_start(out_view[:, :, chunks[i]], result[:])
+
+        def store_last(u, copy):
+            result = keep.tile([P, CHUNK], F32, name=f"last_result{u}")
+            copy(result[:], last[u][:])
+            nc.sync.dma_start(out_view[:, u, chunks[-1]], result[:])
+
+        for i in range(CHUNKS):
+            if i == 2:
+                magnitude_on_vector(1, i)
             else:
-                nc.vector.tensor_copy(result[:], sums[i][:])
-            nc.sync.dma_start(out_view[:, :, cols], result[:])
+                magnitude_on_scalar(1, i)
+        for i in range(CHUNKS):
+            finish(i)
+        store(0, nc.scalar.copy)
+        store(1, nc.vector.tensor_copy)
+        store(2, nc.scalar.copy)
+        store_last(0, nc.vector.tensor_copy)
+        store_last(1, nc.scalar.copy)

@@ -95,8 +95,10 @@ def tile_picked_tokens_store_one_overlay_further_plain_kernel(
 
         feat_s = keep.tile([P, PACK, P], U8, name="feat_s", align_bytes=64)
         feat_w = keep.tile([P, PACK, P], U32, name="feat_w", align_bytes=64)
-        nc.vector.tensor_copy(feat_s[:].rearrange("p t m -> p m t"), wt_s[:].indirect(feat_list[:]))
+        listed_s = keep.tile([P, R], U8, name="listed_s", align_bytes=64)
+        nc.vector.tensor_copy(listed_s[:], wt_s[:].indirect(feat_list[:]))
         nc.vector.tensor_copy(feat_w[:].rearrange("p t m -> p m t"), wt_w[:].indirect(feat_list[:]))
+        nc.vector.tensor_copy(feat_s[:], listed_s[:].rearrange("p (m t) -> p t m", t=PACK))
 
         hidden = [keep.tile([P, J], F32, name=f"hidden{t}") for t in range(PACK)]
         slot_w = keep.tile([P, J], U16, name="slot_w", align_bytes=64)

from contextlib import ExitStack

import concourse.mybir as mybir

K, J, R, T, F, C, S, N = 512, 256, 512, 1024, 1024, 512, 128, 256
FLOPS = 2 * K * R * J + 2 * R * N * C + 2 * K * N * C

F32 = mybir.dt.float32
BF16 = mybir.dt.bfloat16
I32 = mybir.dt.int32
U32 = mybir.dt.uint32
U16 = mybir.dt.uint16
U8 = mybir.dt.uint8
FP8X4 = mybir.dt.float8_e4m3fn_x4
FP4X4 = mybir.dt.float4_e2m1fn_x4
ACT = mybir.ActivationFunctionType
ALU = mybir.AluOpType

P = 128
PACK = 4
QUADS = 4
GROUP = 16
HALF = J // 2
CHUNK = 128
RING = 3
CHUNKS = C // CHUNK


def tile_picked_tokens_store_one_overlay_further_plain_kernel(
    tc, xt_words, xt_scales, wt_words, wt_scales, sa, wb_words, wb_scales, ws_words, ws_scales,
    offs, offs2, offs3, offs4, offs5, offs6, out,
):
    nc = tc.nc
    with ExitStack() as ctx:
        lists = ctx.enter_context(tc.tile_pool(name="lists", bufs=1))
        keep = ctx.enter_context(tc.tile_pool(name="keep", bufs=1))
        psum = ctx.enter_context(tc.psum_pool(name="psum", bufs=1))

        def load_list(src, name):
            tile = lists.tile(list(src.shape), U16, name=name)
            nc.sync.dma_start(tile[:], src)
            return tile

        def cleared_plane(width, name):
            plane = keep.tile([P, width], U8, name=name, align_bytes=64)
            nc.gpsimd.memset(plane[:].bitcast(I32), 0)
            return plane

        def load_scale_rows(plane, scales):
            for q in range(QUADS):
                nc.sync.dma_start(
                    plane[32 * q : 32 * q + 4, :].bitcast(I32), scales[0, 4 * q : 4 * q + 4, :].bitcast(I32)
                )

        def load_scale_window(plane, scales, queues):
            for q, queue in enumerate(queues):
                rows = scales[0, 4 * q : 4 * q + 4, :].bitcast(I32)
                queue.dma_start(
                    plane[32 * q : 32 * q + 32, :].bitcast(I32),
                    rows.unsqueeze(0).broadcast_to([8, 4, scales.shape[2] // 4]),
                )

        wt_s = keep.tile([P, F], U8, name="wt_s", align_bytes=64)
        wt_w = keep.tile([P, F], U32, name="wt_w", align_bytes=64)
        xt_s = keep.tile([P, T], U8, name="xt_s", align_bytes=64)
        xt_w = keep.tile([P, T], U16, name="xt_w", align_bytes=64)
        feat_list = load_list(offs2, "feat_list")
        load_scale_window(wt_s, wt_scales, [nc.scalar, nc.sync, nc.scalar, nc.sync])
        nc.sync.dma_start(wt_w[:].bitcast(I32), wt_words[0].rearrange("p n t -> p (n t)").bitcast(I32))
        nc.sync.dma_start(xt_w[:].bitcast(I32), xt_words[0].bitcast(I32))
        load_scale_window(xt_s, xt_scales, [nc.sync] * QUADS)
        slot_list = load_list(offs, "slot_list")
        board_list = load_list(offs3, "board_list")
        pick_list = load_list(offs4, "pick_list")
        weight = keep.tile([P, PACK], F32, name="weight")
        nc.sync.dma_start(weight[:], sa.rearrange("(p t) o -> p (t o)", t=PACK))
        overlay_list = load_list(offs5, "overlay_list")
        column_list = load_list(offs6, "column_list")

        boards = [keep.tile([P, C], F32, name=f"board{i}") for i in range(RING)]
        overlays = [keep.tile([P, C], F32, name=f"overlay{i}") for i in range(RING)]
        for i in range(RING):
            engine = nc.gpsimd if i == RING - 1 else nc.vector
            engine.memset(boards[i][:], 0.0)
            engine.memset(overlays[i][:], 0.0)

        ws_s = cleared_plane(N, "ws_s")
        wb_s = cleared_plane(N, "wb_s")
        ws_w = keep.tile([P, N], U32, name="ws_w", align_bytes=64)
        nc.sync.dma_start(ws_w[:].bitcast(I32), ws_words[0].rearrange("p n t -> p (n t)").bitcast(I32))
        load_scale_rows(ws_s, ws_scales)
        wb_w = keep.tile([P, N], U16, name="wb_w", align_bytes=64)
        nc.sync.dma_start(wb_w[:].bitcast(I32), wb_words[0].bitcast(I32))
        load_scale_rows(wb_s, wb_scales)

        feat_s = keep.tile([P, PACK, P], U8, name="feat_s", align_bytes=64)
        feat_w = keep.tile([P, PACK, P], U32, name="feat_w", align_bytes=64)
        listed_s = keep.tile([P, R], U8, name="listed_s", align_bytes=64)
        nc.vector.tensor_copy(listed_s[:], wt_s[:].indirect(feat_list[:]))
        nc.vector.tensor_copy(feat_w[:].rearrange("p t m -> p m t"), wt_w[:].indirect(feat_list[:]))
        nc.vector.tensor_copy(feat_s[:], listed_s[:].rearrange("p (m t) -> p t m", t=PACK))

        hidden = [keep.tile([P, J], F32, name=f"hidden{t}") for t in range(PACK)]
        slot_w = keep.tile([P, J], U16, name="slot_w", align_bytes=64)
        slot_s = keep.tile([P, J], U8, name="slot_s", align_bytes=64)

        def hidden_product(t, cols, bank):
            acc = psum.tile([P, cols.stop - cols.start], F32, name=f"acc_{t}_{cols.start}", tag=f"first{bank}")
            nc.tensor.matmul_mx(
                out=acc[:], lhsT=feat_w[:, t, :].bitcast(FP8X4), lhsT_scale=feat_s[:, t, :],
                rhs=slot_w[:, cols].bitcast(FP4X4), rhs_scale=slot_s[:, cols], start=True, stop=True,
            )
            return acc

        halves = [slice(h * HALF, (h + 1) * HALF) for h in range(2)]
        for h, cols in enumerate(halves):
            entries = slot_list[:, cols.start // GROUP : cols.stop // GROUP]
            nc.vector.tensor_copy(slot_w[:, cols], xt_w[:].indirect(entries))
            nc.vector.tensor_copy(slot_s[:, cols], xt_s[:].indirect(entries))
            for t in range(2):
                acc = hidden_product(t, cols, 2 * h + t)
                if h == 0 and t == 0:
                    nc.scalar.copy(hidden[t][:, cols], acc[:])
                else:
                    nc.vector.tensor_copy(hidden[t][:, cols], acc[:])
        for t in range(2, PACK):
            acc = hidden_product(t, slice(0, J), t - 2)
            nc.vector.tensor_copy(hidden[t][:], acc[:])

        col_w = keep.tile([P, C], U16, name="col_w", align_bytes=64)
        col_s = keep.tile([P, C], U8, name="col_s", align_bytes=64)
        nc.vector.tensor_copy(col_w[:], xt_w[:].indirect(column_list[:]))
        nc.vector.tensor_copy(col_s[:], xt_s[:].indirect(column_list[:]))
        chunks = [slice(i * CHUNK, (i + 1) * CHUNK) for i in range(CHUNKS)]
        shared = [psum.tile([P, N // P, CHUNK], F32, name=f"sum{i}") for i in range(CHUNKS - 1)]
        last = [
            psum.tile([P, CHUNK], F32, name="last0", tag="last0"),
            psum.tile([P, CHUNK], F32, name="last1", tag="first2"),
        ]

        def sum_of(i, u):
            return shared[i][:, u, :] if i < CHUNKS - 1 else last[u][:]

        for i, cols in enumerate(chunks):
            for u in range(N // P):
                rows = slice(u * P, (u + 1) * P)
                nc.tensor.matmul_mx(
                    out=sum_of(i, u), lhsT=ws_w[:, rows].bitcast(FP8X4), lhsT_scale=ws_s[:, rows],
                    rhs=col_w[:, cols].bitcast(FP4X4), rhs_scale=col_s[:, cols], start=(u == 0 or i == CHUNKS - 1), stop=False,
                )

        picked = [keep.tile([P, S], F32, name=f"picked{t}") for t in range(PACK)]

        def put_board(t, cols):
            entries = board_list[:, cols.start // GROUP : cols.stop // GROUP]
            nc.scalar.activation(boards[t % RING][:].indirect(entries), hidden[t][:, cols], ACT.Copy)

        def pick(t):
            nc.scalar.activation(
                picked[t][:], hidden[t][:].indirect(pick_list[:]), ACT.Copy, scale=weight[:, t : t + 1]
            )

        def put_overlay(t):
            nc.scalar.activation(overlays[t % RING][:].indirect(overlay_list[:]), picked[t][:], ACT.Copy)

        diffs = [[keep.tile([P, 2, CHUNK], F32, name=f"diff{u}_{i}") for i in range(CHUNKS)] for u in range(2)]
        hid = [keep.tile([P, CHUNK, PACK], BF16, name=f"hid{i}", align_bytes=64) for i in range(CHUNKS)]

        def subtract(t):
            for i, cols in enumerate(chunks):
                nc.vector.tensor_tensor(
                    diffs[t // 2][i][:, t % 2, :], boards[t % RING][:, cols], overlays[t % RING][:, cols], ALU.subtract
                )

        def magnitude_on_vector(u, i):
            pair = diffs[u][i][:].rearrange("p e c -> p c e")
            nc.vector.scalar_tensor_tensor(hid[i][:, :, 2 * u : 2 * u + 2], pair, -1.0, pair, ALU.mult, ALU.max)

        def magnitude_on_scalar(u, i):
            pair = diffs[u][i][:].rearrange("p e c -> p c e")
            nc.scalar.activation(hid[i][:, :, 2 * u : 2 * u + 2], pair, ACT.Abs)

        for cols in halves:
            put_board(0, cols)
            put_board(1, cols)
        pick(0)
        pick(1)
        for t in range(2):
            put_overlay(t)
            subtract(t)
        for i in range(CHUNKS):
            magnitude_on_vector(0, i)
        for t in range(2, PACK):
            pick(t)
            put_board(t, slice(0, J))
            put_overlay(t)
            subtract(t)
        out_view = out.rearrange("(u p) c -> p u c", p=P)

        def finish(i):
            hid_w = keep.tile([P, CHUNK], U32, name=f"hid_w{i}", align_bytes=64)
            hid_s = keep.tile([P, CHUNK], U8, name=f"hid_s{i}", align_bytes=64)
            nc.vector.quantize_mx(
                out=hid_w[:].bitcast(FP8X4), scales=hid_s[:], in_=hid[i][:].rearrange("p c t -> p (c t)")
            )
            for u in range(N // P):
                rows = slice(u * P, (u + 1) * P)
                nc.tensor.matmul_mx(
                    out=sum_of(i, u), lhsT=wb_w[:, rows].bitcast(FP4X4), lhsT_scale=wb_s[:, rows],
                    rhs=hid_w[:].bitcast(FP8X4), rhs_scale=hid_s[:], start=False, stop=(u == N // P - 1 or i == CHUNKS - 1),
                )

        def store(i, copy):
            result = keep.tile([P, N // P, CHUNK], F32, name=f"result{i}")
            copy(result[:], shared[i][:])
            nc.sync.dma_start(out_view[:, :, chunks[i]], result[:])

        def store_last(u, copy):
            result = keep.tile([P, CHUNK], F32, name=f"last_result{u}")
            copy(result[:], last[u][:])
            nc.sync.dma_start(out_view[:, u, chunks[-1]], result[:])

        for i in range(CHUNKS):
            if i == 2:
                magnitude_on_vector(1, i)
            else:
                magnitude_on_scalar(1, i)
        for i in range(CHUNKS):
            finish(i)
        store(0, nc.scalar.copy)
        store(1, nc.vector.tensor_copy)
        store(2, nc.scalar.copy)
        store_last(0, nc.vector.tensor_copy)
        store_last(1, nc.scalar.copy)
